import numpy as np, ml_dtypes
CORES = [242,247,114,119]
N = 4
BF = ml_dtypes.bfloat16
def gentries(a):
    return np.ascontiguousarray(a.reshape(8, 16, -1).transpose(0, 2, 1)).reshape(8, -1)
def gtable(e):
    e = np.asarray(e); return np.ascontiguousarray(e.reshape(8, -1, 16).transpose(0, 2, 1)).reshape(128, -1).astype(np.int32)
V, G, CAP, TH, Q, RO = 1664, 256, 64, 7, 10, 6
H = (N - 1) * G
W = V + H
def near(rng, b, m, C, L):
    k = (rng.random((N, 8, m)) * C).astype(np.int64)
    f = np.take_along_axis(np.broadcast_to(b, (N, 8, 15, 4)), k[:, :, None, :], 3) + rng.integers(-4, 5, (N, 8, 15, m))
    lev = (rng.random((N, 8, m)) * (L + 1)).astype(np.int64)
    return np.concatenate([f & 63, lev[:, :, None]], axis=2)
def parts(rng):
    b = rng.integers(0, 64, (8, 15, 4)); C = rng.integers(1, 4, (N, 8, 1)); L = rng.choice(np.array([2, 3, 5]), (N, 8, 1))
    x = near(rng, b, V, C, L); gx = near(rng, b, H, C, L); c0 = rng.integers(0, 16, (N, 8, V))
    pl = rng.integers(0, W, (N, 8, 16, V)); dr = rng.integers(0, 4, (N, 8, 16, V))
    snd = np.ascontiguousarray(np.argsort(rng.random((N, 8, N - 1, V)), axis=-1)[..., :G])
    return x, gx, c0, pl, dr, snd
def pack(x, gx, c0, pl, dr, snd):
    return {"x": np.ascontiguousarray(x.reshape(N, 128, V)).astype(np.float32).astype(BF), "nb": np.ascontiguousarray((4 * pl + dr).reshape(N, 128, V)).astype(np.int32),
            "gx": np.ascontiguousarray(gx.reshape(N, 128, H)).astype(np.float32).astype(BF), "c0": c0.astype(np.float32).astype(BF),
            "snd": np.stack([gtable(a.reshape(8, -1)) for a in snd])}
def setup_inputs(rng):
    return pack(*parts(rng))
def setup_inputs_room(rng):
    x, gx, c0, pl, dr, snd = parts(rng); u = V // 4; P = rng.integers(16, 48, (8, 15, 1)); C = np.array([0, 1, CAP - 1, CAP, CAP + 1, G])
    first = ((CAP, CAP + 1, G, CAP - 1, 1, 0, CAP, CAP + 1), (CAP, CAP + 1, G, CAP - 1, 2, 1, G, CAP + 1))
    later = (first[0], (0, 0, 1, 0, 1, 0, CAP, CAP))
    watch, slots = {}, {}
    def close(m, g):
        return P[g] + rng.integers(-1, 2, (15, m))
    for q in range(N):
        for g in range(8):
            o = rng.permutation(V); a, b, t, w = o[:u], o[u:2 * u], o[2 * u:3 * u], o[3 * u:]
            watch[q, g] = w; gx[q, g, :15] = close(H, g); gx[q, g, 15] = 1
            x[q, g, 15, a] = rng.integers(20, 64, u); x[q, g, 15, b] = 0; x[q, g, 15, t] = 1; x[q, g, 15, w] = 2
            for part in (b, t, w): x[q, g, :15][:, part] = close(len(part), g)
            pl[q, g][:, a] = b[rng.integers(0, u, (16, u))]; pl[q, g][:, t] = b[rng.integers(0, u, (16, u))]
            c0[q, g, t] = rng.integers(0, 9, u)
            for i in range(int(rng.integers(1, 3))): pl[q, g][c0[q, g, t] + i, t] = a[rng.integers(0, u, u)]
            dr[q, g][:, t] = dr[q, g][:, t] & 1; dr[q, g][:, a[:u // 2]] = 0
            for d in range(N - 1):
                n = int(rng.choice(C)); k = n if rng.random() < 0.5 else min(n, int(rng.choice(C)))
                if q < 2 and d == 0: n, k = first[q][g], later[q][g]
                kind = np.repeat(np.array([2, 1, 0]), np.array([k, n - k, G - n]))
                v = np.concatenate([rng.permutation(a)[:k], rng.permutation(t)[:n - k], rng.permutation(b)[:G - n]])
                s = rng.permutation(G); kind = kind[s]; v = v[s]
                if (q + d + g) % 2 == 0 and 0 < n <= CAP:
                    i = int(np.flatnonzero(kind)[-1]); e = np.array([i, G - 1]); kind[e] = kind[e[::-1]]; v[e] = v[e[::-1]]
                snd[q, g, d] = v; m = np.flatnonzero(kind); z = np.flatnonzero(kind == 2)
                slots[q, g, d] = np.concatenate([np.array([0, G - 1]), m[:1], m[:CAP][-1:], m[CAP:CAP + 1], z[:1], z[-1:], rng.permutation(m)[:8], rng.integers(0, G, 4)]).astype(np.int64)
    for q in range(N):
        for g in range(8):
            w = watch[q, g]; see = np.concatenate([V + d * G + slots[(q - d - 1) % N, g, d] for d in range(N - 1)])
            pl[q, g][c0[q, g, w], w] = see[np.arange(len(w)) % len(see)]
    return pack(x, gx, c0, pl, dr, snd)
def setup_inputs_ties(rng):
    x, gx, c0, pl, dr, snd = parts(rng); b = rng.integers(TH + 1, 63 - TH, (8, 15, 1))
    def edge(m):
        n = Q - 1 + rng.integers(0, 2, (N, 8, 1, m)); k = np.argsort(rng.random((N, 8, 15, m)), axis=2) < n
        root = rng.random((N, 8, 1, m)) < 0.5
        f = b + np.where(root, 0, np.where(k, TH, TH + 1) * (2 * rng.integers(0, 2, (N, 8, 15, m)) - 1))
        return np.concatenate([f, np.where(root, 0, rng.choice(np.array([1, 1, 1, 2]), (N, 8, 1, m)))], axis=2)
    return pack(edge(V), edge(H), c0, pl, dr, snd)
def setup_inputs_ends(rng):
    x, gx, c0, pl, dr, snd = parts(rng)
    c0[:, ::2] = rng.integers(14, 16, (N, 4, V)); c0[:, 1] = 0
    x[:, 2:4, 15] = rng.choice(np.array([0, 62, 62, 63]), (N, 2, V)); gx[:, 2:4, 15] = rng.choice(np.array([61, 62, 63]), (N, 2, H))
    x[:, 4, :15] = 63 * rng.integers(0, 2, (N, 15, V)); dr[:, 5] = 3
    pl[:, 1] = rng.choice(np.array([0, V - 1, V, W - 1]), (N, 16, V)); pl[:, 5] = rng.choice(np.array([0, V - 1, V, W - 1]), (N, 16, V))
    pl[:, 3] = np.arange(V); pl[:, 6] = rng.integers(V, W, (N, 16, V)); pl[:, 7] = pl[:, 7, :1]
    snd[:, ::2] = rng.choice(np.array([0, V - 1, V // 2, 3]), (N, 4, N - 1, G))
    return pack(x, gx, c0, pl, dr, snd)
def setup_inputs_still(rng):
    x, gx, c0, pl, dr, snd = parts(rng); q = rng.permutation(N); a, b = int(q[0]), int(q[1])
    few = rng.permutation(V)[None, :] < CAP // 2
    x[a, :, 15] = np.where(few, np.maximum(x[a, :, 15], 1), 0); x[b, :, 15] = rng.integers(40, 64, (8, V))
    x[:, int(rng.integers(0, 8)), 15] = 0
    return pack(x, gx, c0, pl, dr, snd)
def setup_inputs_spread(rng):
    x, gx, c0, pl, dr, snd = parts(rng)
    def cols(m):
        f = (np.exp2(6 * rng.random((N, 8, 1, m))) * rng.random((N, 8, 15, m))).astype(np.int64)
        return np.minimum(np.concatenate([f, (64 * rng.random((N, 8, 1, m)) ** 3).astype(np.int64)], axis=2), 63)
    pl = np.minimum((W * rng.random(pl.shape) ** 2).astype(np.int64), W - 1); c0 = np.minimum((16 * rng.random(c0.shape) ** 2).astype(np.int64), 15)
    return pack(cols(V), cols(H), c0, pl, dr, snd)
def check_inputs(d):
    bad = []
    for k, hi in (("x", 63), ("gx", 63), ("c0", 15)):
        a = np.asarray(d[k]).astype(np.float32)
        if not np.all((a >= 0) & (a <= hi) & (a == np.floor(a))): bad.append("numbers of " + k)
    for k, hi in (("nb", 4 * W - 1), ("snd", V - 1)):
        if np.min(d[k]) < 0 or np.max(d[k]) > hi: bad.append("range of " + k)
    return bad
def reference(x, nb, gx, c0, snd):
    own = x.astype(np.float32).astype(np.int64).reshape(N, 8, 16, V); gh = gx.astype(np.float32).astype(np.int64).reshape(N, 8, 16, H)
    cur = c0.astype(np.float32).astype(np.int64)
    e = nb.astype(np.int64).reshape(N, 8, 16, V); pl = e >> 2; dr = e & 3
    sl = np.stack([gentries(a) for a in snd]).astype(np.int64).reshape(N, 8, N - 1, G)
    root = own[:, :, 15] == 0
    for s in range(RO):
        p = np.take_along_axis(pl, cur[:, :, None], 2)
        diff = np.take_along_axis(np.concatenate([own, gh], axis=3), p, 3) - own
        votes = np.add.reduce((np.abs(diff[:, :, :15]) <= TH).astype(np.int64), axis=2)
        ok = (votes >= Q) & (diff[:, :, 15] == -1)
        moved = ~ok & ~root
        f, lev = own[:, :, :15], own[:, :, 15]
        f = np.where(ok[:, :, None], f + np.clip(diff[:, :, :15], -1, 1), np.where(moved[:, :, None], (f + dr[:, :, :15]) & 63, f))
        lev = np.where(moved & (cur == 15), np.minimum(lev + 1, 63), lev)
        cur = np.where(moved, (cur + 1) & 15, cur)
        own = np.concatenate([f, lev[:, :, None]], axis=2)
        if s == RO - 1: break
        for a in range(N):
            for t in range(1, N):
                q = (a - t) % N; ix = sl[q, :, t - 1]
                m = np.take_along_axis(moved[q], ix, 1).astype(np.int64); before = np.add.accumulate(m, axis=1) - m
                come = ((m == 1) & (before < CAP))[:, None, :]
                v = np.take_along_axis(own[q], ix[:, None, :], 2)
                gh[a, :, :, (t - 1) * G:t * G] = np.where(come, v, gh[a, :, :, (t - 1) * G:t * G])
    return {"yx": own.reshape(N, 128, V).astype(np.float32).astype(BF), "yc": cur.astype(np.float32)}

import numpy as np
from concourse.bass import DstId, RemoteDMATransfer
from concourse.mybir import AluOpType as A, ActivationFunctionType as F

V, H, W, RO = 1664, 768, 2432, 6
CH, CW, SW = 416, 139, 64
CT = CW + SW
PO, PL = (0, 139, 278), (139, 139, 138)
MAGIC = 1.5 * 2 ** 27 + 16
ROUND = 1.5 * 2 ** 23
GC, PE, FIX, HOP, LINK, LOAD = 1.5, 0.55, 60.0, 150.0, 3200.0, 2200.0
TRIES, SEED = 3000, 0
ON_V = ("01", "02", "03")
MEMO = {}

SCRATCH = {}
for _d, _l in {
    "bfloat16": [("win%d" % i, W) for i in range(RO)] + [("ma%d" % i, 2 * H) for i in range(RO)] + [("win6", V), ("osl", H), ("gxs", H)]
    + [(k, W) for k in ("dd", "near", "sg", "c0a")] + [(k, 48) for k in ("mm", "cs", "o1", "rst", "scs", "scl", "sc0")]
    + [(k, CT) for k in ("cur", "sig", "tt", "ww", "flag", "rootm", "nrt", "inc")] + [("fix", CW), ("fix2", CW), ("wws", 144), ("wwl", 144)]
    + [(k, 384) for k in ("jg", "jc", "e0", "wc", "bc", "br")] + [("drt", 2464), ("sn", V), ("dl", V), ("ow", V)]
    + [(k, 128) for k in ("ib", "nib", "i512", "i384", "i2k", "iw", "i64", "nbd", "bd", "ut")],
    "float32": [("ef", W), ("plr", W), ("base", 48), ("thrw", 48), ("yct", CW), ("pf", 4), ("col", 32), ("jj", 144), ("i32", 128)],
    "float16": [("plc", W), ("mk", W), ("bs16", 48), ("ww1", 144), ("ih", 128), ("i4", 128)],
    "int32": [("nbx", V), ("sndi", 48), ("offi", 152), ("offj", 152), ("pi", 4)],
    "uint16": [("sndu", 48), ("offu", 152), ("mo", 48)],
}.items():
    for _n, _w in _l:
        SCRATCH[_n] = ("sbuf", [128, _w], _d)
for _n in ("Y0", "Y1", "Y2", "Y3", "S0", "S1", "Z", "Wp"):
    SCRATCH[_n] = ("psum", [128, 512], "float32")
SEMAPHORES = (["eV", "eS", "eP", "eG", "sent", "out"] + ["arr%d" % _s for _s in range(RO)] + ["dm%d" % _i for _i in range(7)]
              + ["fl%d" % _i for _i in range(8)] + ["ow%d" % _i for _i in range(4)])


def schedule(ops):
    n = len(ops)
    lastw, readers, sends, pred, hard = {}, {}, {}, [], []
    for i, (q, fn, r, w, sem, t, nm) in enumerate(ops):
        w = [k for k in w if k[0] != "#"]
        raw = set(lastw[k] for k in r if k in lastw)
        oth = set(j for k in w for j in readers.get(k, []) + ([lastw[k]] if k in lastw else [])) - {i}
        h = raw | set(j for j in oth if ops[j][0] != q or ops[j][4] is not None or sem is not None)
        if q == "P":
            h = set(j for j in h if ops[j][0] != "P") | set(lastw[k] for k in r if k[0] == "!" and k in lastw)
        p = dict((j, 0.0) for j in raw | oth)
        for j in h:
            p[j] = HOP + (0.0 if ops[j][4] is None else LOAD) + (60.0 if ops[j][0] == "P" else 0.0)
        for k in r:
            for j in sends.get(k, []):
                p[j] = LINK
        if sem is not None and sem.startswith("to:"):
            sends.setdefault(sem[3:], []).append(i)
        pred.append(p)
        hard.append(h)
        for k in r:
            readers.setdefault(k, []).append(i)
        for k in w:
            lastw[k], readers[k] = i, []
    succ = [[] for _ in range(n)]
    for i in range(n):
        for j in pred[i]:
            succ[j].append(i)
    rank = [0.0] * n
    for i in range(n - 1, -1, -1):
        rank[i] = ops[i][5] + max([rank[k] + pred[k][i] for k in succ[i]] + [0.0])
    bank = [[k for k in o[3] if k[0] == "#"] for o in ops]
    qs, ds = [o[0] for o in ops], [o[5] for o in ops]

    def run(prio):
        left, at, seq = [len(p) for p in pred], [0.0] * n, []
        ready, free, user = dict((q, []) for q in "VSPGY"), dict((q, 0.0) for q in "VSPGY"), {}
        for i in range(n):
            if not left[i]:
                ready[qs[i]].append(i)

        def start(i):
            t = at[i]
            for k in bank[i]:
                for q, e in user.get(k, {}).items():
                    if q != qs[i] and e + HOP + 60.0 > t:
                        t = e + HOP + 60.0
            return t

        for _ in range(n):
            bq, bt = None, 0.0
            for q in "VSPGY":
                if ready[q]:
                    t = max(free[q], min(start(i) for i in ready[q]))
                    if bq is None or t < bt:
                        bq, bt = q, t
            i = max((i for i in ready[bq] if start(i) <= bt), key=lambda i: (prio[i], -i))
            ready[bq].remove(i)
            e = free[bq] = bt + ds[i]
            seq.append(i)
            for k in bank[i]:
                user.setdefault(k, {})[bq] = e
            for k in succ[i]:
                at[k] = max(at[k], e + pred[k][i])
                left[k] -= 1
                if not left[k]:
                    ready[qs[k]].append(k)
        return max(free.values()), seq

    if "order" not in MEMO:
        names = {}
        cls = np.array([names.setdefault(o[6], len(names)) for o in ops])
        rng = np.random.default_rng(SEED)
        shift = np.zeros(len(names))
        cur = best = run(rank)
        for _ in range(TRIES):
            trial = shift + (rng.random(len(names)) < 0.04) * rng.normal(0.0, 2000.0, len(names))
            res = run((np.array(rank) + trial[cls]).tolist())
            if res[0] <= cur[0] + 100.0:
                cur, shift = res, trial
                if res[0] < best[0]:
                    best = res
        MEMO["order"] = best[1]
    order, user = MEMO["order"], {}
    for i in order:
        for k in bank[i]:
            hard[i] |= set(j for q, j in user.get(k, {}).items() if q != ops[i][0])
            user.setdefault(k, {})[ops[i][0]] = i
    pos = dict((i, p) for p, i in enumerate(order))
    seen, waits = {}, {}
    for i in order:
        best = {}
        for j in hard[i]:
            key = ops[j][0] if ops[j][4] is None else j
            if key not in best or pos[j] > pos[best[key]]:
                best[key] = j
        waits[i] = []
        for key, j in best.items():
            if seen.get((ops[i][0], key), -1) < pos[j]:
                seen[(ops[i][0], key)] = pos[j]
                waits[i].append(j)
    return order, waits


def rank_program(g, core, T, topo):
    if T.rank_of(core) is None:
        return
    N = len(T.cores)
    ops, ndma, nsent, c = [], [0], [0], {}
    part = ["setup", 0]

    def op(q, fn, r, w, sem=None, t=130.0):
        part[1] += 1
        ops.append([q, fn, list(r), list(w), sem, t, tuple(part)])

    def vt(n):
        return max(64.0, n) + FIX

    def ts(out, in0, s1, s2, o0, o1, r, w, n=64):
        op("V", lambda: g.vector.tensor_scalar(*([out, in0, s1, s2, o0] + ([] if o1 is None else [o1]))), r, w, None, vt(n))

    def tt(out, a, b, o, r, w, n=64):
        op("V", lambda: g.vector.tensor_tensor(out, a, b, o), r, w, None, vt(n))

    def cp(out, a, r, w, n=64):
        op("V", lambda: g.vector.tensor_copy(out, a), r, w, None, vt(n))

    def act(out, a, f, r, w, bias=0.0, scale=1.0, n=64):
        op("S", lambda: g.scalar.activation(out, a, f, bias=bias, scale=scale), r, w, None, vt(n))

    def mm(out, l, rh, st, sp, r, w, n=64):
        op("P", lambda: g.tensor.matmul(out, l, rh, st, sp), r, w, None, PE * max(n, 64))

    def mms(calls, r, w):
        def fn():
            for i, (out, l, rh, n) in enumerate(calls):
                ins = g.tensor.matmul(out, l, rh, i == 0, i == len(calls) - 1)
            return ins
        op("P", fn, r, w, None, sum(PE * max(x[3], 64) for x in calls))

    def dma(q, out, a, r, w, sem=None):
        if sem is None:
            sem = "dm%d" % ndma[0]
            ndma[0] += 1
        op(q, lambda: (g.sync if q == "Y" else g.scalar).dma_start(out, a), r, w, sem, 100.0)

    def iota(out, pat, base, cm, w, n):
        op("G", lambda: g.iota(out, pat, base, cm, allow_small_or_imprecise_dtypes=True), [], w, None, 130.0 + 2 * n)

    win = [T["win%d" % s] for s in range(RO + 1)]
    ma = [T["ma%d" % s] for s in range(RO)]
    EQ, MUL, ADD, SUB, ID = A.is_equal, A.mult, A.add, A.subtract, F.Identity

    def four(k):
        return [k + str(b) for b in range(4)]

    def own(s):
        return four("win%d." % s)

    def plan(src, sign):
        peers = [(d, T.cores[(T.rank_of(src) + sign * (d + 1)) % N]) for d in range(N - 1)]
        used, out = [], []
        for grp in ([p for p in peers if p[1] not in topo.cores_of(src)], [p for p in peers if p[1] in topo.cores_of(src)]):
            out.append([])
            for i, (d, cc) in enumerate(grp):
                free = [e for e in topo.engines(src, cc) if e not in used]
                k = len(free) // (len(grp) - i)
                while k & (k - 1):
                    k -= 1
                used += free[:k]
                out[-1].append((d, cc, sum(1 << e for e in free[:k]), k))
        return [x for x in out if x]

    def send(grp, src, dst, do, sem, r):
        trs = []
        for d, cc, m, k in grp:
            rid, pid = topo.addr(cc, core)
            trs.append(RemoteDMATransfer(dst_ids=[DstId(rid=rid, pnc=pid)], dma_engine_mask=m, remote_sem=T.sem[sem],
                                         src=src[:, 256 * d:256 * (d + 1)], dst=dst[:, do + 256 * d:do + 256 * (d + 1)]))
            nsent[0] += k
        op("G", lambda: g.remote_dma_fused(trs, local_sem=T.sem.sent), r, [], "to:" + sem, 700.0)

    def arrivals(sign):
        return sum(p[3] for cc in T.cores if cc != core for grp in plan(cc, sign) for p in grp if p[1] == core)

    ext = dict(("arr%d" % s, arrivals(1 if s else -1)) for s in range(RO))

    op("V", lambda: g.vector.memset(T.c0a[:, 0:V], 0.0), [], ["c0a"], None, 900.0)
    dma("Y", T.sndi[:], T.snd[:], [], ["sndi"])
    dma("S", T.nbx[:, 832:V], T.nb[:, 832:V], [], ["nb.2"])
    dma("Y", T.nbx[:, 0:832], T.nb[:, 0:832], [], ["nb.0"])
    dma("S", win[0][:, V:W], T.gx[:], [], ["gx"])
    dma("Y", win[0][:, 0:V], T.x[:], [], own(0))
    dma("Y", T.c0a[0:128:16, 0:V], T.c0[:], ["c0a"], ["c0a"])
    dma("Y", T.ow[:], T.x[:], ["nb.0"], four("ow"))

    op("G", lambda: g.iota(T.pi[:, 0:1], [[0, 1]], 0, 1), [], ["pi0"])
    iota(T.jj[:], [[1, 144]], 0, 0, ["jj"], 144)
    iota(T.jg[:], [[1, 3], [3, 8], [0, 16]], 8, 0, ["jg"], 384)
    iota(T.jc[:], [[0, 24], [1, 16]], 0, 0, ["jc"], 384)
    act(T.gxs[:], win[0][:, V:W], ID, ["gx"], ["gxs"], scale=1.0 / 64, n=H)
    for grp in plan(core, -1):
        send(grp, T.gxs, ma[0], 0, "arr0", ["gxs"])
    iota(T.base[:], [[16, 48]], 0, 1, ["base0"], 48)
    ts(T.pi[:, 1:2], T.pi[:, 0:1], 4, None, A.arith_shift_right, None, ["pi0"], ["pi1"])
    ts(T.pi[:, 2:3], T.pi[:, 0:1], 15, None, A.bitwise_and, None, ["pi0"], ["pi2"])
    ts(T.pi[:, 3:4], T.pi[:, 0:1], 31, None, A.bitwise_and, None, ["pi0"], ["pi3"])
    cp(T.pf[:], T.pi[:], four("pi"), ["pf"])
    for i, k in enumerate(("p", "g", "c", "m")):
        c[k] = T.pf[:, i:i + 1]

    def key(*names):
        return ["pf" if len(k) == 1 else "c." + k for k in names if isinstance(k, str)]

    def val(k):
        return c[k] if isinstance(k, str) else k

    def col(name, src, s1, s2, o0, o1):
        c[name] = T.col[:, len(c):len(c) + 1]
        ts(c[name], c[src], val(s1), val(s2), o0, o1, key(src, s1, s2), key(name))

    def cola(name, src, scale, bias):
        c[name] = T.col[:, len(c):len(c) + 1]
        act(c[name], c[src], ID, key(src), key(name), bias=bias, scale=scale)

    col("lev", "c", 15.0, None, EQ, None)
    col("row0", "c", 0.0, None, EQ, None)
    col("nd", "m", 2.0, None, A.is_lt, None)
    col("dat", "m", 8.0, 2048.0, A.is_ge, MUL)
    col("s2", "c", 15.0, MAGIC, A.not_equal, MUL)
    col("one", "m", 0.0, None, EQ, None)
    col("s1", "s2", 1.0, None, A.max, None)
    for x in (("g16", "g", 16.0, 15.0), ("g24", "g", 3.0, 10.0), ("a0", "m", 10240.0, -4096.0), ("b0", "m", 8192.0, -4096.0),
              ("wsc", "lev", 15.0, 1.0), ("nlev", "lev", -1.0, 1.0), ("drb", "lev", -256.0, -4862.5 / 64),
              ("wb", "dat", -1.0 / 128, 0.0), ("g8", "g", 3.0, 8.0), ("gn", "g", -16.0, 384.0),
              ("t1", "s1", 1.0 / 64, 0.0), ("t2", "s2", 1.0 / 64, 0.0)):
        cola(*x)
    cp(T.sndu[:], T.sndi[:], ["sndi"], ["sndu"])
    col("ac", "a0", "nd", None, MUL, None)
    col("bc", "b0", "nd", None, MUL, None)
    col("hi", "dat", 1.0 / 1024, "one", MUL, ADD)
    act(T.wc[:], T.jc[:], ID, ["jc", "c.ac", "c.bc"], ["wc"], bias=c["ac"], scale=c["bc"], n=384)
    for k, src, n, s1, s2 in (("e0", "jg", 384, "m", None), ("sc0", "jj", 48, "g24", "row0"), ("scl", "jj", 48, "g24", "lev"),
                              ("scs", "jj", 48, "g24", "wsc"), ("wwl", "jj", 144, "g16", "lev"), ("wws", "jj", 144, "g16", "wsc"),
                              ("ww1", "jj", 144, "g16", None), ("ih", "jj", 128, "p", None), ("i4", "jj", 128, "p", -4.0),
                              ("ib", "jj", 128, "p", None), ("bd", "jg", 128, "g8", None)):
        ts(T[k][:], T[src][:, 0:n], val(s1), val(s2), EQ, None if s2 is None else MUL, [src] + key(s1, s2), [k], n)
    ts(T.rst[:], T.jc[:, 0:48], 0.0, None, A.not_equal, None, ["jc"], ["rst"])
    for k, src, x in (("br", "e0", -64.0), ("i32", "ib", 1.0), ("i64", "ib", 1.0 / 64), ("i512", "ib", 512.0), ("nib", "ib", -1.0),
                      ("nbd", "bd", -1.0), ("i384", "ib", 384.0), ("i2k", "ib", 2048.0), ("iw", "ib", "wb")):
        act(T[k][:], T[src][:], ID, [src] + key(x), [k], scale=val(x), n=384 if k == "br" else 128)
    op("G", lambda: g.affine_select(T.ut[:], T.bd[:], [[-1, 128]], A.is_gt, 0.0, 0, 1), ["bd"], ["ut"], None, 430.0)
    act(T.base[:], T.base[:], ID, ["base0", "c.gn"], ["base"], bias=c["gn"])
    cp(T.bs16[:], T.base[:], ["base"], ["bs16"])
    mms([(T.Y0[:, 0:384], T.i2k[:], T.e0[:], 384), (T.Y0[:, 0:384], T.ib[:], T.wc[:], 384)], ["i2k", "e0", "ib", "wc"], ["Y0"])
    act(T.bc[:], T.Y0[:, 0:384], ID, [], ["Y0", "bc"], n=384)

    def thirds(slot):
        return [(k, 64 * k, 64) if slot else (k, PO[k], PL[k]) for k in range(3)]

    def c2_sum(dst0, sc, src, col0, b, slot, r, w):
        mms([(T.Z[32 * b:32 * b + 32, dst0:dst0 + n], T[sc][:, 2 - k:34 - k], src[:, col0 + o:col0 + o + n], n)
             for k, o, n in thirds(slot)], r + [sc], ["#Z", w])

    def c2_bcast(bk, dcol, mat, src, scol, b, slot, last, r):
        for k, o, n in thirds(slot):
            mm(T[bk][:, dcol + o:dcol + o + n], T[mat][32 * b:32 * b + 32, 128 * k:128 * (k + 1)],
               src[32 * b:32 * b + 32, scol:scol + n], False, last and k == 2,
               r + [mat] + (["!" + bk] if slot and b % 2 == 1 and k == 0 else []),
               [bk] + (["!" + bk] if slot and b % 2 == 0 and k == 2 else []), n)

    def wrap(dcol, mat, src, col0, n, r, w):
        mms([(T.Wp[:, dcol:dcol + n], T[mat][:, 15 - k:143 - k], src[:, col0 + k:col0 + 16 * n:16], n) for k in range(16)],
            r + [mat], ["#W", w])

    def os_gather(s):
        for h in range(2):
            act(T.osl[:, 384 * h:384 * (h + 1)], win[s][:, 0:V].indirect(T.sndu[:, 24 * h:24 * (h + 1)]), ID,
                own(s) + ["sndu"], ["os.%d" % h], n=384 * GC)

    def span(slot, b):
        o, n, d = (V + 384 * b, 384, 1696 + 384 * b) if slot else (CH * b, CH, 424 * b)
        return o, n, "%d%d" % (slot, b), T.drt[:, d:d + n]

    def drk(slot, b):
        return ["dr.%d%d" % (slot, b)] + (["fl%d" % (4 + 2 * b), "fl%d" % (5 + 2 * b)] if slot else ["fl%d" % b])

    def select(slot, b):
        o, n, k, _ = span(slot, b)
        bk = "S%d" % (b % 2)
        mm(T[bk][:, 0:n], T.ih[:], T.plc[:, o:o + n], True, False, ["ih", "plc." + k], [bk], n)
        if slot:
            for e in range(2):
                c2_bcast(bk, 192 * e, "bc", T.cur, CW, 2 * b + e, True, e == 1, ["cur.1"])
        else:
            c2_bcast(bk, 0, "bc", T.cur, 0, b, False, True, ["cur.0"])
        ts(T.mk[:, o:o + n], T[bk][:, 0:n], -2048.0, 2048.0, A.max, A.min, [], [bk, "mk." + k], n)

    def finish(slot):
        a, b = (104, 152) if slot else (0, 104)
        k = "off.%d" % slot
        ts(T.offi[:, a:b], T.Wp[:, 96 + a:96 + b], 31936.0, None, ADD, None, ["W.s"] if slot else ["W.m0", "W.m1"], ["#W", k + "i"], b - a)
        ts(T.offj[:, a:b], T.offi[:, a:b], 4095, None, A.bitwise_and, None, [k + "i"], [k + "j"], b - a)
        cp(T.offu[:, a:b], T.offj[:, a:b], [k + "j"], [k], b - a)

    def slot_select():
        select(1, 0)
        select(1, 1)
        wrap(200, "ww1", T.mk, V, 48, ["mk.10", "mk.11"], "W.s")
        finish(1)

    def main_select():
        for h in range(2):
            select(0, 2 * h)
            select(0, 2 * h + 1)
            wrap(96 + 52 * h, "ww1", T.mk, 832 * h, 52, ["mk.0%d" % (2 * h), "mk.0%d" % (2 * h + 1)], "W.m%d" % h)
        finish(0)

    def places(slot, b):
        o, n, k, _ = span(slot, b)
        if slot:
            ts(T.ef[:, o:o + n], T.nbx[:, 0:V].indirect(T.sndu[:, 24 * b:24 * (b + 1)]), -1.5, None, ADD, None,
               ["nb.0", "nb.2", "sndu"], ["ef." + k], n * GC)
        else:
            ts(T.ef[:, o:o + n], T.nbx[:, o:o + n], -1.5, None, ADD, None, ["nb.%d" % (b & 2)], ["ef." + k], n)
        act(T.plr[:, o:o + n], T.ef[:, o:o + n], ID, ["ef." + k], ["plr." + k], bias=ROUND, scale=0.25, n=n)
        ts(T.plc[:, o:o + n], T.plr[:, o:o + n], -(ROUND + 1216.0), None, ADD, None, ["plr." + k], ["plc." + k], n)

    def drift(slot, b):
        o, n, k, dr = span(slot, b)
        bk = "YS"[slot] + str(b)
        mm(T[bk][:, 0:n], T.i32[:], T.ef[:, o:o + n], True, False, ["i32", "ef." + k], [bk], 4 * n)
        mm(T[bk][:, 0:n], T.i4[:], T.plc[:, o:o + n], False, bool(slot), ["i4", "plc." + k], [bk], n)
        if not slot:
            c2_bcast(bk, 0, "br", T.rootm, 0, b, False, True, ["root"])
        act(dr, T[bk][:, 0:n], F.Relu, ["c.drb"], [bk] + drk(slot, b), bias=c["drb"], scale=1.0 / 64, n=n)

    def cursors(s, slot):
        a, n, k = CW * slot, (CW, SW)[slot], str(slot)
        cs, sk = slice(a, a + n), ["sig.s"] if slot else four("sig.")
        z, z2 = T.Z[:, CT + a:CT + a + n], T.Wp[:, 300 + a:300 + a + n]
        two = [(T.ib[:], T.cur[:, cs], n), (T.nib[:], T.sig[:, cs], n)]
        mms([(z,) + x for x in two], ["ib", "nib", "cur." + k] + sk, ["#Z", "Z.c" + k])
        act(T.ww[:, cs], z, F.Sign, ["Z.c" + k], ["#Z", "ww." + k], bias=s - 32.5, n=n)
        mms([(z2,) + x for x in two + [(T.iw[:], T.ww[:, cs], n)]], ["ib", "nib", "iw", "cur." + k, "ww." + k] + sk, ["#W", "W.c" + k])
        act(T.cur[:, cs], z2, ID, ["c.wb", "W.c" + k], ["#W", "cur." + k], bias=c["wb"], n=n)

    def flags(s, slot):
        a, n, k = CW * slot, (CW, SW)[slot], str(slot)
        z = T.Z[:, CT + a:CT + a + n]
        mms([(z, T.ib[:], T.cur[:, a:a + n], n), (z, T.ib[:], T.inc[:, a:a + n], n)], ["ib", "cur." + k, "inc"], ["#Z", "Z.c" + k])
        act(T.flag[:, a:a + n], z, F.Relu, ["Z.c" + k], ["#Z", "flag." + k], bias=(s / 2.0 - 15.0) / 64, scale=1.0 / 128, n=n)
        for b in range(4):
            d, f = (1696 + 192 * b, "fl%d" % (4 + b)) if slot else (424 * b, "fl%d" % b)
            dma("Y", T.drt[15:128:16, d:d + 3 * n], T.flag[32 * b + 8:32 * b + 32, a:a + n], ["flag." + k], [f], f)

    def near(s, o, n, r, w):
        x, y = ("t1", "t2") if s else ("s1", "s2")
        ts(T.near[:, o:o + n], T.dd[:, o:o + n], c[x], c[y], ADD, EQ, r + key(x, y), w, n / 2)

    def decide(s, b):
        cs, bk, rows = slice(CH * b, CH * (b + 1)), "Y%d" % b, slice(32 * b, 32 * b + 32)
        tt(T.dd[:, cs], win[s][:, 0:W].indirect(T.offu[:, 26 * b:26 * (b + 1)]), T.ow[:, cs],
           SUB, own(s) + ["arr%d" % s if s else "gx", "off.0", "ow%d" % b], ["d.%d" % b], CH * GC)
        act(T.sn[:, cs], T.dd[:, cs], F.Sign, ["d.%d" % b, "c.nlev"], ["sn.%d" % b], scale=c["nlev"], n=CH)
        near(s, CH * b, CH, ["d.%d" % b], ["n.%d" % b])
        c2_sum(0, "scs", T.near, CH * b, b, False, ["n.%d" % b], "Z.%d" % b)
        act(T.sig[rows, 0:CW], T.Z[rows, 0:CW], F.Sign, ["Z.%d" % b], ["#Z", "sig.%d" % b], bias=-25.5, n=CW)
        mm(T[bk][:, 0:CH], T.i64[:], T.sn[:, cs], True, False, ["i64", "sn.%d" % b], [bk], CH)
        c2_bcast(bk, 0, "e0", T.sig, 0, b, False, True, ["sig.%d" % b])

    def mod(s, bk, o, n, k, a, d, r, out, wk):
        bank, sg, r = T[bk][:, 0:n], T.sg[:, o:o + n], r + ["ib", "i64"]
        two = [(bank, (T.ib if s else T.i64)[:], a, n), (bank, T.ib[:], d, n)]
        mms(two, r, [bk])
        act(sg, bank, F.Sigmoid, [], [bk, "sg." + k], bias=-63.5 * 512, scale=32768.0, n=n)
        if k in ON_V and s < RO - 1:
            tt(out, bank, sg, SUB, ["sg." + k], [bk, wk], n)
        else:
            mms(two + [(bank, T.nib[:], sg, n)], r + ["nib", "sg." + k], [bk])
            act(out, bank, ID, [], [bk, wk], scale=64.0 if s == RO - 1 else 1.0, n=n)

    def update(s, b):
        o, n, k, dr = span(0, b)
        cs, bk, wk = slice(o, o + n), "Y%d" % b, "win%d.%d" % (s + 1, b)
        tt(T.dl[:, cs], T[bk][:, 0:n], dr, A.max, drk(0, b), [bk, "dl." + k], n)
        mod(s, bk, o, n, k, win[s][:, cs], T.dl[:, cs], ["win%d.%d" % (s, b), "dl." + k], win[s + 1][:, cs], wk)
        if s == RO - 1:
            dma("Y", T.yx[:, cs], win[s + 1][:, cs], [wk], [], "out")
        else:
            dma("Y", T.ow[:, cs], win[s + 1][:, cs], [wk], ["ow%d" % b], "ow%d" % b)

    def slots(s):
        if s:
            os_gather(s)
        for h in range(2):
            o, n, k, dr = span(1, h)
            oh = T.osl[:, 384 * h:384 * (h + 1)]
            tt(T.dd[:, o:o + n], win[s][:, 0:W].indirect(T.offu[:, 104 + 24 * h:128 + 24 * h]), oh, SUB,
               own(s) + ["arr%d" % s if s else "gx", "off.1", "os.%d" % h], ["d.s%d" % h], 384 * GC)
            mod(s, "S%d" % h, o, n, k, oh, dr, ["os.%d" % h] + drk(1, h), ma[s][:, H + 384 * h:H + 384 * (h + 1)], "ma%d.a%d" % (s, h))
        near(s, V, H, ["d.s0", "d.s1"], ["n.s"])
        wrap(0, "wws", T.near, V, 48, ["n.s"], "W.n")
        tt(T.mm[:], T.Wp[:, 0:48], T.thrw[:], A.is_lt, ["thrw", "W.n"], ["#W", "mm"])
        op("V", lambda: g.vector.tensor_tensor_scan(T.cs[:], T.rst[:], T.mm[:], 0.0, MUL, ADD), ["rst", "mm"], ["cs"])
        p1, p2 = T.Wp[:, 48:96], T.Wp[:, 248:296]
        mms([(p1, T.ut[:], T.mm[:], 48), (p1, T.i512[:], T.mm[:], 48), (p1, T.nbd[:], T.cs[:], 48)],
            ["ut", "i512", "nbd", "mm", "cs"], ["#W", "W.p"])
        act(T.o1[:], p1, F.Sign, ["W.p"], ["#W", "o1"], bias=-447.5)
        mms([(p2, T.ih[:], T.bs16[:], 48), (p2, T.i384[:], T.o1[:], 48)], ["ih", "bs16", "i384", "o1"], ["#W", "W.o"])
        cp(T.mo[:], p2, ["W.o"], ["#W", "mo"])
        mk = ["ma%d.m%d" % (s, d) for d in range(3)] if s else ["arr0"]
        for grp in plan(core, 1):
            lo, hi = grp[0][0], grp[-1][0] + 1
            wk = ["ma%d.m%d" % (s + 1, d) for d in range(lo, hi)]
            act(ma[s + 1][:, 256 * lo:256 * hi], ma[s][:, :].indirect(T.mo[:, 16 * lo:16 * hi]), ID,
                mk + ["mo", "ma%d.a0" % s, "ma%d.a1" % s], wk, n=256 * GC * (hi - lo))
            send(grp, ma[s + 1], win[s + 1], V, "arr%d" % (s + 1), wk)
        if s < RO - 2:
            for b in range(4):
                c2_sum(CW, "scs", T.near, V + 192 * b, b, True, ["n.s"], "Z.s%d" % b)
            act(T.sig[:, CW:CT], T.Z[:, CW:CT], F.Sign, four("Z.s"), ["#Z", "sig.s"], bias=-25.5)
            cursors(s, 1)
            flags(s + 1, 1)

    os_gather(0)
    act(T.c0a[:, V:W], T.c0a[:, 0:V].indirect(T.sndu[:]), ID, ["c0a", "sndu"], ["c0s"], n=H * GC)
    for b in range(4):
        c2_sum(CT, "scl", win[0], CH * b, b, False, own(0), "Z.l%d" % b)
        c2_sum(0, "sc0", T.c0a, CH * b, b, False, ["c0a"], "Z.%d" % b)
        c2_sum(CT + CW, "scl", T.osl, 192 * b, b, True, ["os.0", "os.1"], "Z.m%d" % b)
        c2_sum(CW, "sc0", T.c0a, V + 192 * b, b, True, ["c0s"], "Z.s%d" % b)
    wrap(0, "wwl", T.osl, 0, 48, ["os.0", "os.1"], "W.n")
    ts(T.nrt[:], T.Z[:, CT:2 * CT], 0.0, None, A.is_gt, None, four("Z.l") + four("Z.m"), ["#Z", "nrt"], CT)
    ts(T.inc[:], T.Z[:, CT:2 * CT], 63.0, -128.0, EQ, MUL, four("Z.l") + four("Z.m"), ["#Z", "inc"], CT)
    tt(T.tt[:], T.Z[:, 0:CT], T.nrt[:], MUL, ["nrt"] + four("Z.") + four("Z.s"), ["#Z", "tt"], CT)
    act(T.fix[:], T.Z[:, 0:CW], ID, four("Z."), ["#Z", "fix"], bias=-6.0, n=CW)
    ts(T.thrw[:], T.Wp[:, 0:48], 1.0, 25.5, A.min, MUL, ["W.n"], ["#W", "thrw"])
    ts(T.cur[:], T.tt[:], 2.0, c["hi"], MUL, ADD, ["tt", "c.hi"], ["cur.0", "cur.1"], CT / 2)
    act(T.rootm[:], T.nrt[:], ID, ["nrt"], ["root"], bias=1.0, scale=-1.0, n=CT)
    tt(T.fix2[:], T.fix[:], T.rootm[:, 0:CW], MUL, ["fix", "root"], ["fix2"], 2 * CW)
    places(1, 0)
    places(1, 1)
    slot_select()
    drift(1, 0)
    drift(1, 1)
    flags(0, 1)
    for b in range(4):
        places(0, b)
        drift(0, b)
    flags(0, 0)

    for s in range(RO):
        part[:] = ["slots", 0 if s else 2]
        if s < RO - 1:
            slots(s)
        part[:] = ["first", 0]
        if s == 0:
            main_select()
        part[:] = ["ssel", 0]
        if s < RO - 2:
            slot_select()
        part[:] = ["decide", 0]
        for b in range(4):
            decide(s, b)
        cursors(s, 0)
        part[:] = ["update" if s < RO - 1 else "end", 0]
        for b in range(4):
            update(s, b)
        part[:] = ["msel" if s < RO - 1 else "last", 0]
        if s < RO - 1:
            flags(s + 1, 0)
            main_select()
        else:
            ts(T.yct[:], T.cur[:, 0:CW], 0.5, 2.0, MUL, ADD, ["cur.0"], ["yc0"], CW)
            tt(T.yct[:], T.yct[:], T.fix2[:], ADD, ["yc0", "fix2"], ["yct"], 2 * CW)
            for b in range(4):
                for k, o, n in thirds(0):
                    dma("Y", T.yc[:, CH * b + o:CH * b + o + n], T.yct[32 * b + 8 + k:32 * b + 32:3, 0:n], ["yct"], [], "out")

    order, waits = schedule(ops)
    need = set(j for i in order for j in waits[i])
    eng = {"V": g.vector, "S": g.scalar, "P": g.tensor, "G": g, "Y": g.sync}
    cnt, tok, waited = {}, {}, set()
    for i in order:
        q, fn, r, w, sem, t, nm = ops[i]
        for j in waits[i]:
            eng[q].wait_ge(T.sem[tok[j][0]], tok[j][1])
        for k in r:
            if k in ext and (q, k) not in waited:
                waited.add((q, k))
                eng[q].wait_ge(T.sem[k], ext[k])
        ins = fn()
        if (sem is None and i in need) or (sem is not None and not sem.startswith("to:")):
            name, k = ("e" + q, 1) if sem is None else (sem, 16)
            cnt[name] = cnt.get(name, 0) + k
            ins.then_inc(T.sem[name], k)
            tok[i] = (name, cnt[name])
    g.sync.wait_ge(T.sem.out, cnt["out"])
    g.wait_ge(T.sem.sent, nsent[0])
